import numpy as np
import ml_dtypes


def mxq(x, axis, fmt="e4m3"):
    dtype, down = {"e4m3": (ml_dtypes.float8_e4m3fn, 7), "e5m2": (ml_dtypes.float8_e5m2, 14)}[fmt]
    v = np.moveaxis(np.asarray(x, np.float32).astype(ml_dtypes.bfloat16).astype(np.float64), axis, -1)
    blocks = v.reshape(v.shape[:-1] + (-1, 32))
    amax = np.abs(blocks).max(-1, keepdims=True)
    byte = np.maximum(np.where(amax > 0, np.frexp(amax)[1] - 1 + 127, 0) - down, 1)
    scale = np.exp2(byte - 127.0)
    codes = (blocks / scale).astype(np.float32).astype(dtype).astype(np.float64)
    return np.moveaxis((codes * scale).reshape(v.shape), -1, axis)


WIDE = False


def mx_kscale(k):
    if not WIDE:
        return np.ones(k)
    levels = np.array([30, -30])
    if k % 512:
        return np.exp2(np.random.permutation(np.resize(levels, k // 32))).repeat(32)
    a = np.empty((k // 512, 16))
    for p in range(k // 512):
        a[p, :8] = np.random.permutation(np.resize(levels, 8))
        for g in range(8):
            far = levels[np.abs(levels - a[p, g]) >= 10]
            a[p, g + 8] = far[np.random.randint(len(far))]
    return np.exp2(a.ravel()).repeat(32)


def f64(x):
    return np.asarray(x).astype(np.float64)


def striped(idx):
    return np.tile(np.asarray(idx).reshape(-1, 16).T, (8, 1)).astype(np.uint16)


def unstriped(offs):
    return offs[:16].T.reshape(-1).astype(np.int64)


E2M1 = np.array([0.0, 0.5, 1.0, 1.5, 2.0, 3.0, 4.0, 6.0, -0.0, -0.5, -1.0, -1.5, -2.0, -3.0, -4.0, -6.0])


def pack_weight(w, fmt):
    k, n = w.shape
    w = f64(np.asarray(w, np.float32).astype(ml_dtypes.bfloat16)).reshape(k // 32, 32, n)
    amax = np.abs(w).max(1)
    if fmt in ("e4m3", "e5m2"):
        byte = np.frexp(amax)[1] - 1 + 127 - (7 if fmt == "e4m3" else 14)
    else:
        mant, ex = np.frexp(amax / 6.0)
        byte = np.where(mant > 0.5, ex, ex - 1) + 127
    byte = np.clip(np.where(amax > 0, byte, 1), 1, 254)
    scaled = (w * np.exp2(127.0 - byte)[:, None, :]).reshape(k, n).astype(np.float32)
    by_word = np.ascontiguousarray(scaled.reshape(k // 512, 128, 4, n).transpose(0, 1, 3, 2))
    if fmt in ("e4m3", "e5m2"):
        words = by_word.astype(ml_dtypes.float8_e4m3fn if fmt == "e4m3" else ml_dtypes.float8_e5m2).view(np.uint8)
    else:
        c = by_word.astype(ml_dtypes.float4_e2m1fn).view(np.uint8) & 0xF
        words = (c[..., 0::2] | (c[..., 1::2] << 4)).reshape(k // 512, 128, 2 * n)
    return np.ascontiguousarray(words), np.ascontiguousarray(byte.astype(np.uint8).reshape(k // 512, 16, n))


def unpack_weight(words, scales, fmt):
    g, _, n = scales.shape
    words = np.ascontiguousarray(words).reshape(g, 128, n, -1)
    if fmt in ("e4m3", "e5m2"):
        vals = words.view(ml_dtypes.float8_e4m3fn if fmt == "e4m3" else ml_dtypes.float8_e5m2).astype(np.float64)
    else:
        nib = np.empty((g, 128, n, 4), np.uint8)
        nib[..., 0::2] = words & 0xF
        nib[..., 1::2] = words >> 4
        vals = E2M1[nib]
    vals = vals * np.repeat(np.exp2(scales.astype(np.float64) - 127.0), 8, axis=1)[..., None]
    return vals.transpose(0, 1, 3, 2).reshape(g * 512, n)


K, J, N, R, T, V = 512, 512, 256, 256, 1024, 1024


def setup_inputs():
    n = np.random.standard_normal
    idx = np.random.permutation(T)[:J]
    idx2 = np.random.permutation(V)[:J]
    fj = mx_kscale(J)
    fk = mx_kscale(K)
    drp = pack_weight(n((K, R)) * 1 / np.sqrt(K) / fk[:, None], "e5m2")
    return {
        "xf": (n((K, T))).astype(np.float32),
        "ra": (np.random.uniform(0.5, 1.5, (1, J)) * fj).astype(np.float32),
        "lo": (np.random.uniform(-0.3, 0.5, (K, 1))).astype(np.float32),
        "gt": (n((N, V)) * np.exp(0.5 * n((1, V)))).astype(np.float32),
        "rb": (np.random.uniform(0.5, 1.5, (1, J)) / fj).astype(np.float32),
        "sv": (n((N, V))).astype(np.float32),
        "fkr": (np.random.uniform(0.5, 1.5, (1, K)) * fk).astype(np.float32),
        "dr_words": drp[0],
        "dr_scales": drp[1],
        "old": (12.0 * n((R, N))).astype(np.float32),
        "offs": striped(idx),
        "offs2": striped(idx2),
    }


def reference(xf, ra, lo, gt, rb, sv, fkr, dr_words, dr_scales, old, offs, offs2):
    idx = unstriped(offs)
    idx2 = unstriped(offs2)
    dru = unpack_weight(dr_words, dr_scales, "e5m2")
    us = np.maximum(f64(xf)[:, idx] - f64(lo), 0.0) * f64(ra)
    ut = us.T
    uj = ut * f64(fkr)
    gs = f64(gt)[:, idx2] * np.maximum(f64(sv)[:, idx2], 0.0) * f64(rb)
    gj = gs.T
    ujq = mxq(uj, 0, "e4m3")
    gjq = mxq(gj, 0, "e5m2")
    w = ujq.T @ gjq
    wq = mxq(w, 0, "e5m2")
    v2 = dru.T @ wq
    y = 0.05 * np.maximum(v2, f64(old))
    return y

@@ -1,0 +1,239 @@
+from contextlib import ExitStack
+
+import concourse.mybir as mybir
+from concourse.masks import make_identity
+
+K, J, N, R, T, V = 512, 512, 256, 256, 1024, 1024
+FLOPS = 2 * J * K * N + 2 * K * R * N
+
+F32 = mybir.dt.float32
+BF16 = mybir.dt.bfloat16
+U32 = mybir.dt.uint32
+I32 = mybir.dt.int32
+U16 = mybir.dt.uint16
+U8 = mybir.dt.uint8
+E4M3 = mybir.dt.float8_e4m3fn_x4
+E5M2 = mybir.dt.float8_e5m2_x4
+ALU = mybir.AluOpType
+COPY = mybir.ActivationFunctionType.Copy
+
+P = 128
+PACK = 4
+HALVES = 2
+LIST_COLS = J // 16
+X3_COLS, SV0_COLS, GT1_COLS = 12, 12, 10
+
+
+def tile_list_directions_over_saved_larger_kernel(tc, xf, ra, lo, gt, rb, sv, fkr, dr_words, dr_scales, old, offs, offs2, out):
+    nc = tc.nc
+    with ExitStack() as ctx:
+        lists = ctx.enter_context(tc.tile_pool(name="lists", bufs=1))
+        sb = ctx.enter_context(tc.tile_pool(name="sb", bufs=1))
+        ps = ctx.enter_context(tc.psum_pool(name="ps", bufs=1))
+
+        offs2_sb = lists.tile([P, LIST_COLS], U16, name="offs2_sb")
+        offs_sb = lists.tile([P, LIST_COLS], U16, name="offs_sb")
+        rb_sb = sb.tile([P, PACK], F32, name="rb_sb")
+        ra_sb = sb.tile([P, PACK], F32, name="ra_sb")
+        fk_sb = sb.tile([P, PACK], F32, name="fk_sb")
+        lo_sb = sb.tile([P, PACK], F32, name="lo_sb")
+        sv_sb = [sb.tile([P, V], F32, name=f"sv{h}") for h in range(HALVES)]
+        gt_sb = [sb.tile([P, V], F32, name=f"gt{h}") for h in range(HALVES)]
+        xf_sb = [sb.tile([P, T], F32, name=f"xf{t}") for t in range(PACK)]
+        dr_codes = sb.tile([P, R], U32, name="dr_codes", align_bytes=64)
+        dr_plane = sb.tile([P, R], U8, name="dr_plane", align_bytes=64)
+        old_sb = sb.tile([P, HALVES, N], F32, name="old_sb")
+
+        ident = sb.tile([P, P], F32, name="ident")
+        make_identity(nc, ident[:])
+        nc.gpsimd.memset(dr_plane[:].bitcast(I32), 0)
+
+        xf_rows = xf.rearrange("(p t) c -> p t c", t=PACK)
+        nc.sync.dma_start(out=fk_sb[:], in_=fkr.rearrange("o (p i) -> p (o i)", i=PACK))
+        nc.sync.dma_start(out=lo_sb[:], in_=lo.rearrange("(p i) o -> p (i o)", i=PACK))
+        nc.sync.dma_start(out=ra_sb[:], in_=ra.rearrange("o (p i) -> p (o i)", i=PACK))
+        nc.sync.dma_start(out=xf_sb[0][:], in_=xf_rows[:, 0, :])
+        nc.sync.dma_start(offs_sb[:], offs)
+        nc.sync.dma_start(out=xf_sb[1][:], in_=xf_rows[:, 1, :])
+        nc.sync.dma_start(out=rb_sb[:], in_=rb.rearrange("o (p i) -> p (o i)", i=PACK))
+        nc.sync.dma_start(offs2_sb[:], offs2)
+        for t in range(2, PACK):
+            nc.sync.dma_start(out=xf_sb[t][:], in_=xf_rows[:, t, :])
+        for h in range(HALVES):
+            nc.sync.dma_start(out=sv_sb[h][:], in_=sv[h * P : (h + 1) * P, :])
+        for h in range(HALVES):
+            nc.sync.dma_start(out=gt_sb[h][:], in_=gt[h * P : (h + 1) * P, :])
+        nc.sync.dma_start(out=old_sb[:], in_=old.rearrange("(h p) n -> p h n", p=P))
+        nc.sync.dma_start(out=dr_codes[:].bitcast(I32), in_=dr_words[0].rearrange("p n t -> p (n t)").bitcast(I32))
+        for q in range(4):
+            nc.sync.dma_start(
+                out=dr_plane[32 * q : 32 * q + 4, :].bitcast(I32), in_=dr_scales[0, 4 * q : 4 * q + 4, :].bitcast(I32)
+            )
+
+        def overlaid(name, cols):
+            both = sb.tile([P, 2 * J - 16 * cols], F32, name=name)
+            return both[:, 0:J], both[:, J - 16 * cols : 2 * J - 16 * cols]
+
+        def plain(name, tag=None):
+            one = sb.tile([P, J], F32, name=name, tag=tag or name)
+            return one[:]
+
+        factor0, x_pick3 = overlaid("factor0_xpick3", X3_COLS)
+        factor1, sv_pick0 = overlaid("factor1_svpick0", SV0_COLS)
+        sv_pick1, gt_pick1 = overlaid("svpick1_gtpick1", GT1_COLS)
+        factor = [factor0, factor1, plain("factor2"), plain("factor3")]
+        x_pick = [plain("x_pick0"), plain("x_pick1"), plain("x_pick2"), x_pick3]
+        sv_pick = [sv_pick0, sv_pick1]
+        gt_pick = [plain("gt_pick0"), gt_pick1]
+
+        def pick(picked, window, offsets, vector_cols):
+            nc.scalar.activation(picked[:, 16 * vector_cols : J], window[:].indirect(offsets[:, vector_cols:LIST_COLS]), COPY)
+
+        def pick_share(picked, window, offsets, vector_cols):
+            if vector_cols > 0:
+                nc.vector.tensor_copy(picked[:, 0 : 16 * vector_cols], window[:].indirect(offsets[:, 0:vector_cols]))
+
+        fk_ps = ps.tile([P, PACK, P], F32, name="fk_ps", tag="bankF")
+        for t in range(PACK):
+            nc.tensor.transpose(fk_ps[:, t, :], fk_sb[:, t : t + 1].to_broadcast([P, P]), ident[:])
+        neg_lo = sb.tile([P, PACK], F32, name="neg_lo")
+        nc.scalar.activation(neg_lo[:], lo_sb[:], COPY, scale=-1.0)
+        for t in range(PACK):
+            nc.vector.tensor_tensor(
+                out=factor[t].rearrange("p (m i) -> p m i", i=PACK),
+                in0=fk_ps[:, t, :].unsqueeze(2).to_broadcast([P, P, PACK]),
+                in1=ra_sb[:].unsqueeze(1).to_broadcast([P, P, PACK]),
+                op=ALU.mult,
+            )
+        x_ps = [ps.tile([P, PACK, P], F32, name=f"x_ps{t}", tag=f"bankX{t}") for t in range(PACK)]
+
+        def open_features(t):
+            for i in range(PACK):
+                nc.tensor.matmul(
+                    x_ps[t][:, i, :], neg_lo[:, t : t + 1].to_broadcast([P, P]), ident[:],
+                    start=(i == 0), stop=False, is_transpose=True,
+                )
+
+        def turn_features(t):
+            for i in range(PACK):
+                nc.tensor.matmul(
+                    x_ps[t][:, i, :], x_pick[t][:, i:J:PACK], ident[:], start=False, stop=(i == PACK - 1), is_transpose=True
+                )
+
+        u_codes, u_plane = [], []
+
+        def finish_features(t):
+            uj = sb.tile([P, P, PACK], BF16, name=f"uj{t}", align_bytes=64)
+            nc.vector.scalar_tensor_tensor(
+                out=uj[:], in0=x_ps[t][:].rearrange("p i m -> p m i"), scalar=0.0,
+                in1=factor[t].rearrange("p (m i) -> p m i", i=PACK), op0=ALU.max, op1=ALU.mult,
+            )
+            codes = sb.tile([P, P], U32, name=f"u_codes{t}", align_bytes=64)
+            plane = sb.tile([P, P], U8, name=f"u_plane{t}", align_bytes=64)
+            nc.vector.quantize_mx(out=codes[:].bitcast(E4M3), scales=plane[:], in_=uj[:].rearrange("p m i -> p (m i)"))
+            u_codes.append(codes)
+            u_plane.append(plane)
+
+        def make_gate(h):
+            gate_h = plain(f"gate{h}", tag=f"factor{2 + h}")
+            nc.vector.scalar_tensor_tensor(
+                out=gate_h.rearrange("q (p i) -> q p i", i=PACK), in0=sv_pick[h].rearrange("q (p i) -> q p i", i=PACK),
+                scalar=0.0, in1=rb_ps[:].rearrange("q i p -> q p i"), op0=ALU.max, op1=ALU.mult,
+            )
+            return gate_h
+
+        for t in range(PACK):
+            open_features(t)
+        for t in range(3):
+            pick(x_pick[t], xf_sb[t], offs_sb, 0)
+        pick(x_pick[3], xf_sb[3], offs_sb, X3_COLS)
+        pick(sv_pick[0], sv_sb[0], offs2_sb, SV0_COLS)
+        pick(sv_pick[1], sv_sb[1], offs2_sb, 0)
+        pick(gt_pick[0], gt_sb[0], offs2_sb, 0)
+        pick(gt_pick[1], gt_sb[1], offs2_sb, GT1_COLS)
+        turn_features(0)
+        finish_features(0)
+        pick_share(x_pick[3], xf_sb[3], offs_sb, X3_COLS)
+        turn_features(1)
+        finish_features(1)
+        pick_share(sv_pick[0], sv_sb[0], offs2_sb, SV0_COLS)
+        rb_ps = ps.tile([P, PACK, P], F32, name="rb_ps", tag="bankR")
+        for i in range(PACK):
+            nc.tensor.transpose(rb_ps[:, i, :], rb_sb[:, i : i + 1].to_broadcast([P, P]), ident[:])
+        turn_features(2)
+        finish_features(2)
+        gate = [make_gate(0)]
+        turn_features(3)
+        finish_features(3)
+        gate.append(make_gate(1))
+
+        def turn_gradients(h):
+            pairs = (sv_pick[1], x_pick[0])[h][:, 0 : J // 2]
+            nc.vector.tensor_tensor(pairs.bitcast(BF16), gt_pick[h], gate[h], ALU.mult)
+            g_ps = ps.tile([P, 2, P], F32, name=f"g_ps{h}", tag=("bankF", "bankX0")[h])
+            for u in range(2):
+                nc.tensor.transpose(g_ps[:, u, :], pairs[:, u : J // 2 : 2], ident[:])
+            gj = sb.tile([P, P * PACK], BF16, name=f"gj{h}", align_bytes=64)
+            nc.scalar.copy(
+                out=gj[:].bitcast(F32).rearrange("p (n u) -> p n u", u=2), in_=g_ps[:].rearrange("p u n -> p n u")
+            )
+            return gj
+
+        def first_product(h, gj):
+            g_codes = sb.tile([P, P], U32, name=f"g_codes{h}", align_bytes=64)
+            g_plane = sb.tile([P, P], U8, name=f"g_plane{h}", align_bytes=64)
+            nc.vector.quantize_mx(out=g_codes[:].bitcast(E5M2), scales=g_plane[:], in_=gj[:])
+            w_ps = ps.tile([P, PACK, P], F32, name=f"w_ps{h}", tag=f"bankW{h}")
+            for t in range(PACK):
+                nc.tensor.matmul_mx(
+                    out=w_ps[:, t, :],
+                    lhsT=u_codes[t][:].bitcast(E4M3), lhsT_scale=u_plane[t][:],
+                    rhs=g_codes[:].bitcast(E5M2), rhs_scale=g_plane[:],
+                    start=True, stop=True,
+                )
+            return w_ps
+
+        def round_moment(h, w_ps):
+            w_bf = sb.tile([P, P, PACK], BF16, name=f"w_bf{h}", align_bytes=64)
+            nc.scalar.copy(out=w_bf[:], in_=w_ps[:].rearrange("p t n -> p n t"))
+            return w_bf
+
+        def second_product(h, w_bf):
+            w_codes = sb.tile([P, P], U32, name=f"w_codes{h}", align_bytes=64)
+            w_plane = sb.tile([P, P], U8, name=f"w_plane{h}", align_bytes=64)
+            nc.vector.quantize_mx(
+                out=w_codes[:].bitcast(E5M2), scales=w_plane[:], in_=w_bf[:].rearrange("p n t -> p (n t)")
+            )
+            v_ps = ps.tile([P, HALVES, P], F32, name=f"v_ps{h}", tag=f"bankX{h + 1}")
+            for rh in range(HALVES):
+                nc.tensor.matmul_mx(
+                    out=v_ps[:, rh, :],
+                    lhsT=dr_codes[:, rh * P : (rh + 1) * P].bitcast(E5M2), lhsT_scale=dr_plane[:, rh * P : (rh + 1) * P],
+                    rhs=w_codes[:].bitcast(E5M2), rhs_scale=w_plane[:],
+                    start=True, stop=True,
+                )
+            return v_ps
+
+        out_rows = out.rearrange("(h p) n -> p h n", p=P)
+
+        def store(h, v_ps):
+            res = sb.tile([P, HALVES, P], F32, name=f"res{h}")
+            nc.vector.scalar_tensor_tensor(
+                out=res[:], in0=v_ps[:], scalar=0.05, in1=old_scaled[:, :, h * P : (h + 1) * P],
+                op0=ALU.mult, op1=ALU.max,
+            )
+            nc.sync.dma_start(out=out_rows[:, :, h * P : (h + 1) * P], in_=res[:])
+
+        pick_share(gt_pick[1], gt_sb[1], offs2_sb, GT1_COLS)
+        gj0 = turn_gradients(0)
+        gj1 = turn_gradients(1)
+        w_ps0 = first_product(0, gj0)
+        old_scaled = sb.tile([P, HALVES, N], F32, name="old_scaled", tag="gj0", align_bytes=64)
+        nc.vector.tensor_scalar(out=old_scaled[:], in0=old_sb[:], scalar1=0.05, scalar2=None, op0=ALU.mult)
+        w_ps1 = first_product(1, gj1)
+        w_bf0 = round_moment(0, w_ps0)
+        w_bf1 = round_moment(1, w_ps1)
+        v_ps0 = second_product(0, w_bf0)
+        v_ps1 = second_product(1, w_bf1)
+        store(0, v_ps0)
+        store(1, v_ps1)

@@ -21,7 +21,8 @@ P = 128
 PACK = 4
 HALVES = 2
 LIST_COLS = J // 16
-X3_COLS, SV0_COLS, GT1_COLS = 12, 12, 10
+X1_COLS = 12
+X3_COLS, SV0_COLS, GT1_COLS = 8, 12, 10
 
 
 def tile_list_directions_over_saved_larger_kernel(tc, xf, ra, lo, gt, rb, sv, fkr, dr_words, dr_scales, old, offs, offs2, out):
@@ -34,7 +35,8 @@ def tile_list_directions_over_saved_larger_kernel(tc, xf, ra, lo, gt, rb, sv, fk
         offs2_sb = lists.tile([P, LIST_COLS], U16, name="offs2_sb")
         offs_sb = lists.tile([P, LIST_COLS], U16, name="offs_sb")
         rb_sb = sb.tile([P, PACK], F32, name="rb_sb")
-        ra_sb = sb.tile([P, PACK], F32, name="ra_sb")
+        x_pick1 = sb.tile([P, J], F32, name="x_pick1", align_bytes=64)
+        ra_sb = x_pick1[:, 0:PACK]
         fk_sb = sb.tile([P, PACK], F32, name="fk_sb")
         lo_sb = sb.tile([P, PACK], F32, name="lo_sb")
         sv_sb = [sb.tile([P, V], F32, name=f"sv{h}") for h in range(HALVES)]
@@ -49,13 +51,13 @@ def tile_list_directions_over_saved_larger_kernel(tc, xf, ra, lo, gt, rb, sv, fk
         nc.gpsimd.memset(dr_plane[:].bitcast(I32), 0)
 
         xf_rows = xf.rearrange("(p t) c -> p t c", t=PACK)
-        nc.sync.dma_start(out=fk_sb[:], in_=fkr.rearrange("o (p i) -> p (o i)", i=PACK))
-        nc.sync.dma_start(out=lo_sb[:], in_=lo.rearrange("(p i) o -> p (i o)", i=PACK))
-        nc.sync.dma_start(out=ra_sb[:], in_=ra.rearrange("o (p i) -> p (o i)", i=PACK))
+        nc.scalar.dma_start(out=fk_sb[:], in_=fkr.rearrange("o (p i) -> p (o i)", i=PACK))
+        nc.scalar.dma_start(out=lo_sb[:], in_=lo.rearrange("(p i) o -> p (i o)", i=PACK))
+        nc.scalar.dma_start(out=ra_sb, in_=ra.rearrange("o (p i) -> p (o i)", i=PACK))
         nc.sync.dma_start(out=xf_sb[0][:], in_=xf_rows[:, 0, :])
         nc.sync.dma_start(offs_sb[:], offs)
         nc.sync.dma_start(out=xf_sb[1][:], in_=xf_rows[:, 1, :])
-        nc.sync.dma_start(out=rb_sb[:], in_=rb.rearrange("o (p i) -> p (o i)", i=PACK))
+        nc.gpsimd.dma_start(out=rb_sb[:], in_=rb.rearrange("o (p i) -> p (o i)", i=PACK))
         nc.sync.dma_start(offs2_sb[:], offs2)
         for t in range(2, PACK):
             nc.sync.dma_start(out=xf_sb[t][:], in_=xf_rows[:, t, :])
@@ -75,14 +77,14 @@ def tile_list_directions_over_saved_larger_kernel(tc, xf, ra, lo, gt, rb, sv, fk
             return both[:, 0:J], both[:, J - 16 * cols : 2 * J - 16 * cols]
 
         def plain(name, tag=None):
-            one = sb.tile([P, J], F32, name=name, tag=tag or name)
+            one = sb.tile([P, J], F32, name=name, tag=tag or name, align_bytes=64)
             return one[:]
 
         factor0, x_pick3 = overlaid("factor0_xpick3", X3_COLS)
         factor1, sv_pick0 = overlaid("factor1_svpick0", SV0_COLS)
         sv_pick1, gt_pick1 = overlaid("svpick1_gtpick1", GT1_COLS)
         factor = [factor0, factor1, plain("factor2"), plain("factor3")]
-        x_pick = [plain("x_pick0"), plain("x_pick1"), plain("x_pick2"), x_pick3]
+        x_pick = [plain("x_pick0"), x_pick1[:], plain("x_pick2"), x_pick3]
         sv_pick = [sv_pick0, sv_pick1]
         gt_pick = [plain("gt_pick0"), gt_pick1]
 
@@ -97,12 +99,12 @@ def tile_list_directions_over_saved_larger_kernel(tc, xf, ra, lo, gt, rb, sv, fk
         for t in range(PACK):
             nc.tensor.transpose(fk_ps[:, t, :], fk_sb[:, t : t + 1].to_broadcast([P, P]), ident[:])
         neg_lo = sb.tile([P, PACK], F32, name="neg_lo")
-        nc.scalar.activation(neg_lo[:], lo_sb[:], COPY, scale=-1.0)
+        nc.vector.tensor_scalar(out=neg_lo[:], in0=lo_sb[:], scalar1=-1.0, scalar2=None, op0=ALU.mult)
         for t in range(PACK):
             nc.vector.tensor_tensor(
                 out=factor[t].rearrange("p (m i) -> p m i", i=PACK),
                 in0=fk_ps[:, t, :].unsqueeze(2).to_broadcast([P, P, PACK]),
-                in1=ra_sb[:].unsqueeze(1).to_broadcast([P, P, PACK]),
+                in1=ra_sb.unsqueeze(1).to_broadcast([P, P, PACK]),
                 op=ALU.mult,
             )
         x_ps = [ps.tile([P, PACK, P], F32, name=f"x_ps{t}", tag=f"bankX{t}") for t in range(PACK)]
@@ -120,19 +122,23 @@ def tile_list_directions_over_saved_larger_kernel(tc, xf, ra, lo, gt, rb, sv, fk
                     x_ps[t][:, i, :], x_pick[t][:, i:J:PACK], ident[:], start=False, stop=(i == PACK - 1), is_transpose=True
                 )
 
+        uj = [sb.tile([P, 2, P * PACK], BF16, name=f"uj{a}", align_bytes=64) for a in range(2)]
         u_codes, u_plane = [], []
 
         def finish_features(t):
-            uj = sb.tile([P, P, PACK], BF16, name=f"uj{t}", align_bytes=64)
             nc.vector.scalar_tensor_tensor(
-                out=uj[:], in0=x_ps[t][:].rearrange("p i m -> p m i"), scalar=0.0,
+                out=uj[t // 2][:, t % 2, :].rearrange("p (m i) -> p m i", i=PACK),
+                in0=x_ps[t][:].rearrange("p i m -> p m i"), scalar=0.0,
                 in1=factor[t].rearrange("p (m i) -> p m i", i=PACK), op0=ALU.max, op1=ALU.mult,
             )
-            codes = sb.tile([P, P], U32, name=f"u_codes{t}", align_bytes=64)
-            plane = sb.tile([P, P], U8, name=f"u_plane{t}", align_bytes=64)
-            nc.vector.quantize_mx(out=codes[:].bitcast(E4M3), scales=plane[:], in_=uj[:].rearrange("p m i -> p (m i)"))
-            u_codes.append(codes)
-            u_plane.append(plane)
+
+        def quantize_features(a, tag):
+            codes = sb.tile([P, 2 * P], U32, name=f"u_codes{a}", tag=tag, align_bytes=64)
+            plane = sb.tile([P, 2 * P], U8, name=f"u_plane{a}", align_bytes=64)
+            nc.vector.quantize_mx(out=codes[:].bitcast(E4M3), scales=plane[:], in_=uj[a][:].rearrange("p t c -> p (t c)"))
+            for t in range(2):
+                u_codes.append(codes[:, t * P : (t + 1) * P])
+                u_plane.append(plane[:, t * P : (t + 1) * P])
 
         def make_gate(h):
             gate_h = plain(f"gate{h}", tag=f"factor{2 + h}")
@@ -145,7 +151,8 @@ def tile_list_directions_over_saved_larger_kernel(tc, xf, ra, lo, gt, rb, sv, fk
         for t in range(PACK):
             open_features(t)
         for t in range(3):
-            pick(x_pick[t], xf_sb[t], offs_sb, 0)
+            pick(x_pick[t], xf_sb[t], offs_sb, X1_COLS if t == 1 else 0)
+        pick_share(x_pick[1], xf_sb[1], offs_sb, X1_COLS)
         pick(x_pick[3], xf_sb[3], offs_sb, X3_COLS)
         pick(sv_pick[0], sv_sb[0], offs2_sb, SV0_COLS)
         pick(sv_pick[1], sv_sb[1], offs2_sb, 0)
@@ -157,6 +164,7 @@ def tile_list_directions_over_saved_larger_kernel(tc, xf, ra, lo, gt, rb, sv, fk
         turn_features(1)
         finish_features(1)
         pick_share(sv_pick[0], sv_sb[0], offs2_sb, SV0_COLS)
+        quantize_features(0, "u_codes0")
         rb_ps = ps.tile([P, PACK, P], F32, name="rb_ps", tag="bankR")
         for i in range(PACK):
             nc.tensor.transpose(rb_ps[:, i, :], rb_sb[:, i : i + 1].to_broadcast([P, P]), ident[:])
@@ -187,7 +195,7 @@ def tile_list_directions_over_saved_larger_kernel(tc, xf, ra, lo, gt, rb, sv, fk
             for t in range(PACK):
                 nc.tensor.matmul_mx(
                     out=w_ps[:, t, :],
-                    lhsT=u_codes[t][:].bitcast(E4M3), lhsT_scale=u_plane[t][:],
+                    lhsT=u_codes[t].bitcast(E4M3), lhsT_scale=u_plane[t],
                     rhs=g_codes[:].bitcast(E5M2), rhs_scale=g_plane[:],
                     start=True, stop=True,
                 )
@@ -227,6 +235,7 @@ def tile_list_directions_over_saved_larger_kernel(tc, xf, ra, lo, gt, rb, sv, fk
         pick_share(gt_pick[1], gt_sb[1], offs2_sb, GT1_COLS)
         gj0 = turn_gradients(0)
         gj1 = turn_gradients(1)
+        quantize_features(1, "factor3")
         w_ps0 = first_product(0, gj0)
         old_scaled = sb.tile([P, HALVES, N], F32, name="old_scaled", tag="gj0", align_bytes=64)
         nc.vector.tensor_scalar(out=old_scaled[:], in0=old_sb[:], scalar1=0.05, scalar2=None, op0=ALU.mult)

@@ -54,10 +54,10 @@ def tile_list_directions_over_saved_larger_kernel(tc, xf, ra, lo, gt, rb, sv, fk
         nc.scalar.dma_start(out=fk_sb[:], in_=fkr.rearrange("o (p i) -> p (o i)", i=PACK))
         nc.scalar.dma_start(out=lo_sb[:], in_=lo.rearrange("(p i) o -> p (i o)", i=PACK))
         nc.scalar.dma_start(out=ra_sb, in_=ra.rearrange("o (p i) -> p (o i)", i=PACK))
-        nc.sync.dma_start(out=xf_sb[0][:], in_=xf_rows[:, 0, :])
+        nc.scalar.dma_start(out=rb_sb[:], in_=rb.rearrange("o (p i) -> p (o i)", i=PACK))
         nc.sync.dma_start(offs_sb[:], offs)
+        nc.sync.dma_start(out=xf_sb[0][:], in_=xf_rows[:, 0, :])
         nc.sync.dma_start(out=xf_sb[1][:], in_=xf_rows[:, 1, :])
-        nc.gpsimd.dma_start(out=rb_sb[:], in_=rb.rearrange("o (p i) -> p (o i)", i=PACK))
         nc.sync.dma_start(offs2_sb[:], offs2)
         for t in range(2, PACK):
             nc.sync.dma_start(out=xf_sb[t][:], in_=xf_rows[:, t, :])
@@ -99,7 +99,7 @@ def tile_list_directions_over_saved_larger_kernel(tc, xf, ra, lo, gt, rb, sv, fk
         for t in range(PACK):
             nc.tensor.transpose(fk_ps[:, t, :], fk_sb[:, t : t + 1].to_broadcast([P, P]), ident[:])
         neg_lo = sb.tile([P, PACK], F32, name="neg_lo")
-        nc.vector.tensor_scalar(out=neg_lo[:], in0=lo_sb[:], scalar1=-1.0, scalar2=None, op0=ALU.mult)
+        nc.scalar.activation(neg_lo[:], lo_sb[:], COPY, scale=-1.0)
         for t in range(PACK):
             nc.vector.tensor_tensor(
                 out=factor[t].rearrange("p (m i) -> p m i", i=PACK),

@@ -21,8 +21,7 @@ P = 128
 PACK = 4
 HALVES = 2
 LIST_COLS = J // 16
-X1_COLS = 12
-X3_COLS, SV0_COLS, GT1_COLS = 8, 12, 10
+X1_COLS, SV0_COLS, GT1_COLS = 8, 10, 12
 
 
 def tile_list_directions_over_saved_larger_kernel(tc, xf, ra, lo, gt, rb, sv, fkr, dr_words, dr_scales, old, offs, offs2, out):
@@ -51,13 +50,13 @@ def tile_list_directions_over_saved_larger_kernel(tc, xf, ra, lo, gt, rb, sv, fk
         nc.gpsimd.memset(dr_plane[:].bitcast(I32), 0)
 
         xf_rows = xf.rearrange("(p t) c -> p t c", t=PACK)
-        nc.scalar.dma_start(out=fk_sb[:], in_=fkr.rearrange("o (p i) -> p (o i)", i=PACK))
-        nc.scalar.dma_start(out=lo_sb[:], in_=lo.rearrange("(p i) o -> p (i o)", i=PACK))
-        nc.scalar.dma_start(out=ra_sb, in_=ra.rearrange("o (p i) -> p (o i)", i=PACK))
-        nc.scalar.dma_start(out=rb_sb[:], in_=rb.rearrange("o (p i) -> p (o i)", i=PACK))
-        nc.sync.dma_start(offs_sb[:], offs)
+        nc.sync.dma_start(out=fk_sb[:], in_=fkr.rearrange("o (p i) -> p (o i)", i=PACK))
+        nc.sync.dma_start(out=lo_sb[:], in_=lo.rearrange("(p i) o -> p (i o)", i=PACK))
+        nc.sync.dma_start(out=ra_sb, in_=ra.rearrange("o (p i) -> p (o i)", i=PACK))
         nc.sync.dma_start(out=xf_sb[0][:], in_=xf_rows[:, 0, :])
+        nc.sync.dma_start(offs_sb[:], offs)
         nc.sync.dma_start(out=xf_sb[1][:], in_=xf_rows[:, 1, :])
+        nc.sync.dma_start(out=rb_sb[:], in_=rb.rearrange("o (p i) -> p (o i)", i=PACK))
         nc.sync.dma_start(offs2_sb[:], offs2)
         for t in range(2, PACK):
             nc.sync.dma_start(out=xf_sb[t][:], in_=xf_rows[:, t, :])
@@ -72,28 +71,28 @@ def tile_list_directions_over_saved_larger_kernel(tc, xf, ra, lo, gt, rb, sv, fk
                 out=dr_plane[32 * q : 32 * q + 4, :].bitcast(I32), in_=dr_scales[0, 4 * q : 4 * q + 4, :].bitcast(I32)
             )
 
-        def overlaid(name, cols):
-            both = sb.tile([P, 2 * J - 16 * cols], F32, name=name)
-            return both[:, 0:J], both[:, J - 16 * cols : 2 * J - 16 * cols]
+        def chained(name, overlaps):
+            starts = [0]
+            for cols in overlaps:
+                starts.append(starts[-1] + J - 16 * cols)
+            whole = sb.tile([P, starts[-1] + J], F32, name=name)
+            return [whole[:, s : s + J] for s in starts]
 
         def plain(name, tag=None):
             one = sb.tile([P, J], F32, name=name, tag=tag or name, align_bytes=64)
             return one[:]
 
-        factor0, x_pick3 = overlaid("factor0_xpick3", X3_COLS)
-        factor1, sv_pick0 = overlaid("factor1_svpick0", SV0_COLS)
-        sv_pick1, gt_pick1 = overlaid("svpick1_gtpick1", GT1_COLS)
-        factor = [factor0, factor1, plain("factor2"), plain("factor3")]
-        x_pick = [plain("x_pick0"), x_pick1[:], plain("x_pick2"), x_pick3]
-        sv_pick = [sv_pick0, sv_pick1]
+        factor1, sv_pick0, gt_pick1 = chained("factor1_svpick0_gtpick1", [SV0_COLS, GT1_COLS])
+        factor = [plain("factor0"), factor1, plain("factor2"), plain("factor3")]
+        x_pick = [plain("x_pick0"), x_pick1[:], plain("x_pick2"), plain("x_pick3")]
+        sv_pick = [sv_pick0, plain("sv_pick1")]
         gt_pick = [plain("gt_pick0"), gt_pick1]
 
         def pick(picked, window, offsets, vector_cols):
             nc.scalar.activation(picked[:, 16 * vector_cols : J], window[:].indirect(offsets[:, vector_cols:LIST_COLS]), COPY)
 
         def pick_share(picked, window, offsets, vector_cols):
-            if vector_cols > 0:
-                nc.vector.tensor_copy(picked[:, 0 : 16 * vector_cols], window[:].indirect(offsets[:, 0:vector_cols]))
+            nc.vector.tensor_copy(picked[:, 0 : 16 * vector_cols], window[:].indirect(offsets[:, 0:vector_cols]))
 
         fk_ps = ps.tile([P, PACK, P], F32, name="fk_ps", tag="bankF")
         for t in range(PACK):
@@ -150,17 +149,14 @@ def tile_list_directions_over_saved_larger_kernel(tc, xf, ra, lo, gt, rb, sv, fk
 
         for t in range(PACK):
             open_features(t)
-        for t in range(3):
+        for t in range(PACK):
             pick(x_pick[t], xf_sb[t], offs_sb, X1_COLS if t == 1 else 0)
         pick_share(x_pick[1], xf_sb[1], offs_sb, X1_COLS)
-        pick(x_pick[3], xf_sb[3], offs_sb, X3_COLS)
         pick(sv_pick[0], sv_sb[0], offs2_sb, SV0_COLS)
         pick(sv_pick[1], sv_sb[1], offs2_sb, 0)
         pick(gt_pick[0], gt_sb[0], offs2_sb, 0)
-        pick(gt_pick[1], gt_sb[1], offs2_sb, GT1_COLS)
         turn_features(0)
         finish_features(0)
-        pick_share(x_pick[3], xf_sb[3], offs_sb, X3_COLS)
         turn_features(1)
         finish_features(1)
         pick_share(sv_pick[0], sv_sb[0], offs2_sb, SV0_COLS)
@@ -171,12 +167,13 @@ def tile_list_directions_over_saved_larger_kernel(tc, xf, ra, lo, gt, rb, sv, fk
         turn_features(2)
         finish_features(2)
         gate = [make_gate(0)]
+        pick(gt_pick[1], gt_sb[1], offs2_sb, GT1_COLS)
         turn_features(3)
         finish_features(3)
         gate.append(make_gate(1))
 
         def turn_gradients(h):
-            pairs = (sv_pick[1], x_pick[0])[h][:, 0 : J // 2]
+            pairs = x_pick[2 * h][:, 0 : J // 2]
             nc.vector.tensor_tensor(pairs.bitcast(BF16), gt_pick[h], gate[h], ALU.mult)
             g_ps = ps.tile([P, 2, P], F32, name=f"g_ps{h}", tag=("bankF", "bankX0")[h])
             for u in range(2):

from contextlib import ExitStack

import concourse.mybir as mybir
from concourse.masks import make_identity

K, J, N, R, T, V = 512, 512, 256, 256, 1024, 1024
FLOPS = 2 * J * K * N + 2 * K * R * N

F32 = mybir.dt.float32
BF16 = mybir.dt.bfloat16
U32 = mybir.dt.uint32
I32 = mybir.dt.int32
U16 = mybir.dt.uint16
U8 = mybir.dt.uint8
E4M3 = mybir.dt.float8_e4m3fn_x4
E5M2 = mybir.dt.float8_e5m2_x4
ALU = mybir.AluOpType
COPY = mybir.ActivationFunctionType.Copy

P = 128
PACK = 4
HALVES = 2
LIST_COLS = J // 16
X1_COLS, SV0_COLS, GT1_COLS = 8, 10, 12


def tile_list_directions_over_saved_larger_kernel(tc, xf, ra, lo, gt, rb, sv, fkr, dr_words, dr_scales, old, offs, offs2, out):
    nc = tc.nc
    with ExitStack() as ctx:
        lists = ctx.enter_context(tc.tile_pool(name="lists", bufs=1))
        sb = ctx.enter_context(tc.tile_pool(name="sb", bufs=1))
        ps = ctx.enter_context(tc.psum_pool(name="ps", bufs=1))

        offs2_sb = lists.tile([P, LIST_COLS], U16, name="offs2_sb")
        offs_sb = lists.tile([P, LIST_COLS], U16, name="offs_sb")
        rb_sb = sb.tile([P, PACK], F32, name="rb_sb")
        x_pick1 = sb.tile([P, J], F32, name="x_pick1", align_bytes=64)
        ra_sb = x_pick1[:, 0:PACK]
        fk_sb = sb.tile([P, PACK], F32, name="fk_sb")
        lo_sb = sb.tile([P, PACK], F32, name="lo_sb")
        sv_sb = [sb.tile([P, V], F32, name=f"sv{h}") for h in range(HALVES)]
        gt_sb = [sb.tile([P, V], F32, name=f"gt{h}") for h in range(HALVES)]
        xf_sb = [sb.tile([P, T], F32, name=f"xf{t}") for t in range(PACK)]
        dr_codes = sb.tile([P, R], U32, name="dr_codes", align_bytes=64)
        dr_plane = sb.tile([P, R], U8, name="dr_plane", align_bytes=64)
        old_sb = sb.tile([P, HALVES, N], F32, name="old_sb")

        ident = sb.tile([P, P], F32, name="ident")
        make_identity(nc, ident[:])
        nc.gpsimd.memset(dr_plane[:].bitcast(I32), 0)

        xf_rows = xf.rearrange("(p t) c -> p t c", t=PACK)
        nc.sync.dma_start(out=fk_sb[:], in_=fkr.rearrange("o (p i) -> p (o i)", i=PACK))
        nc.sync.dma_start(out=lo_sb[:], in_=lo.rearrange("(p i) o -> p (i o)", i=PACK))
        nc.sync.dma_start(out=ra_sb, in_=ra.rearrange("o (p i) -> p (o i)", i=PACK))
        nc.sync.dma_start(out=xf_sb[0][:], in_=xf_rows[:, 0, :])
        nc.sync.dma_start(offs_sb[:], offs)
        nc.sync.dma_start(out=xf_sb[1][:], in_=xf_rows[:, 1, :])
        nc.sync.dma_start(out=rb_sb[:], in_=rb.rearrange("o (p i) -> p (o i)", i=PACK))
        nc.sync.dma_start(offs2_sb[:], offs2)
        for t in range(2, PACK):
            nc.sync.dma_start(out=xf_sb[t][:], in_=xf_rows[:, t, :])
        for h in range(HALVES):
            nc.sync.dma_start(out=sv_sb[h][:], in_=sv[h * P : (h + 1) * P, :])
        for h in range(HALVES):
            nc.sync.dma_start(out=gt_sb[h][:], in_=gt[h * P : (h + 1) * P, :])
        nc.sync.dma_start(out=old_sb[:], in_=old.rearrange("(h p) n -> p h n", p=P))
        nc.sync.dma_start(out=dr_codes[:].bitcast(I32), in_=dr_words[0].rearrange("p n t -> p (n t)").bitcast(I32))
        for q in range(4):
            nc.sync.dma_start(
                out=dr_plane[32 * q : 32 * q + 4, :].bitcast(I32), in_=dr_scales[0, 4 * q : 4 * q + 4, :].bitcast(I32)
            )

        def chained(name, overlaps):
            starts = [0]
            for cols in overlaps:
                starts.append(starts[-1] + J - 16 * cols)
            whole = sb.tile([P, starts[-1] + J], F32, name=name)
            return [whole[:, s : s + J] for s in starts]

        def plain(name, tag=None):
            one = sb.tile([P, J], F32, name=name, tag=tag or name, align_bytes=64)
            return one[:]

        factor1, sv_pick0, gt_pick1 = chained("factor1_svpick0_gtpick1", [SV0_COLS, GT1_COLS])
        factor = [plain("factor0"), factor1, plain("factor2"), plain("factor3")]
        x_pick = [plain("x_pick0"), x_pick1[:], plain("x_pick2"), plain("x_pick3")]
        sv_pick = [sv_pick0, plain("sv_pick1")]
        gt_pick = [plain("gt_pick0"), gt_pick1]

        def pick(picked, window, offsets, vector_cols):
            nc.scalar.activation(picked[:, 16 * vector_cols : J], window[:].indirect(offsets[:, vector_cols:LIST_COLS]), COPY)

        def pick_share(picked, window, offsets, vector_cols):
            nc.vector.tensor_copy(picked[:, 0 : 16 * vector_cols], window[:].indirect(offsets[:, 0:vector_cols]))

        fk_ps = ps.tile([P, PACK, P], F32, name="fk_ps", tag="bankF")
        for t in range(PACK):
            nc.tensor.transpose(fk_ps[:, t, :], fk_sb[:, t : t + 1].to_broadcast([P, P]), ident[:])
        neg_lo = sb.tile([P, PACK], F32, name="neg_lo")
        nc.scalar.activation(neg_lo[:], lo_sb[:], COPY, scale=-1.0)
        for t in range(PACK):
            nc.vector.tensor_tensor(
                out=factor[t].rearrange("p (m i) -> p m i", i=PACK),
                in0=fk_ps[:, t, :].unsqueeze(2).to_broadcast([P, P, PACK]),
                in1=ra_sb.unsqueeze(1).to_broadcast([P, P, PACK]),
                op=ALU.mult,
            )
        x_ps = [ps.tile([P, PACK, P], F32, name=f"x_ps{t}", tag=f"bankX{t}") for t in range(PACK)]

        def open_features(t):
            for i in range(PACK):
                nc.tensor.matmul(
                    x_ps[t][:, i, :], neg_lo[:, t : t + 1].to_broadcast([P, P]), ident[:],
                    start=(i == 0), stop=False, is_transpose=True,
                )

        def turn_features(t):
            for i in range(PACK):
                nc.tensor.matmul(
                    x_ps[t][:, i, :], x_pick[t][:, i:J:PACK], ident[:], start=False, stop=(i == PACK - 1), is_transpose=True
                )

        uj = [sb.tile([P, 2, P * PACK], BF16, name=f"uj{a}", align_bytes=64) for a in range(2)]
        u_codes, u_plane = [], []

        def finish_features(t):
            nc.vector.scalar_tensor_tensor(
                out=uj[t // 2][:, t % 2, :].rearrange("p (m i) -> p m i", i=PACK),
                in0=x_ps[t][:].rearrange("p i m -> p m i"), scalar=0.0,
                in1=factor[t].rearrange("p (m i) -> p m i", i=PACK), op0=ALU.max, op1=ALU.mult,
            )

        def quantize_features(a, tag):
            codes = sb.tile([P, 2 * P], U32, name=f"u_codes{a}", tag=tag, align_bytes=64)
            plane = sb.tile([P, 2 * P], U8, name=f"u_plane{a}", align_bytes=64)
            nc.vector.quantize_mx(out=codes[:].bitcast(E4M3), scales=plane[:], in_=uj[a][:].rearrange("p t c -> p (t c)"))
            for t in range(2):
                u_codes.append(codes[:, t * P : (t + 1) * P])
                u_plane.append(plane[:, t * P : (t + 1) * P])

        def make_gate(h):
            gate_h = plain(f"gate{h}", tag=f"factor{2 + h}")
            nc.vector.scalar_tensor_tensor(
                out=gate_h.rearrange("q (p i) -> q p i", i=PACK), in0=sv_pick[h].rearrange("q (p i) -> q p i", i=PACK),
                scalar=0.0, in1=rb_ps[:].rearrange("q i p -> q p i"), op0=ALU.max, op1=ALU.mult,
            )
            return gate_h

        for t in range(PACK):
            open_features(t)
        for t in range(PACK):
            pick(x_pick[t], xf_sb[t], offs_sb, X1_COLS if t == 1 else 0)
        pick_share(x_pick[1], xf_sb[1], offs_sb, X1_COLS)
        pick(sv_pick[0], sv_sb[0], offs2_sb, SV0_COLS)
        pick(sv_pick[1], sv_sb[1], offs2_sb, 0)
        pick(gt_pick[0], gt_sb[0], offs2_sb, 0)
        turn_features(0)
        finish_features(0)
        turn_features(1)
        finish_features(1)
        pick_share(sv_pick[0], sv_sb[0], offs2_sb, SV0_COLS)
        quantize_features(0, "u_codes0")
        rb_ps = ps.tile([P, PACK, P], F32, name="rb_ps", tag="bankR")
        for i in range(PACK):
            nc.tensor.transpose(rb_ps[:, i, :], rb_sb[:, i : i + 1].to_broadcast([P, P]), ident[:])
        turn_features(2)
        finish_features(2)
        gate = [make_gate(0)]
        pick(gt_pick[1], gt_sb[1], offs2_sb, GT1_COLS)
        turn_features(3)
        finish_features(3)
        gate.append(make_gate(1))

        def turn_gradients(h):
            pairs = x_pick[2 * h][:, 0 : J // 2]
            nc.vector.tensor_tensor(pairs.bitcast(BF16), gt_pick[h], gate[h], ALU.mult)
            g_ps = ps.tile([P, 2, P], F32, name=f"g_ps{h}", tag=("bankF", "bankX0")[h])
            for u in range(2):
                nc.tensor.transpose(g_ps[:, u, :], pairs[:, u : J // 2 : 2], ident[:])
            gj = sb.tile([P, P * PACK], BF16, name=f"gj{h}", align_bytes=64)
            nc.scalar.copy(
                out=gj[:].bitcast(F32).rearrange("p (n u) -> p n u", u=2), in_=g_ps[:].rearrange("p u n -> p n u")
            )
            return gj

        def first_product(h, gj):
            g_codes = sb.tile([P, P], U32, name=f"g_codes{h}", align_bytes=64)
            g_plane = sb.tile([P, P], U8, name=f"g_plane{h}", align_bytes=64)
            nc.vector.quantize_mx(out=g_codes[:].bitcast(E5M2), scales=g_plane[:], in_=gj[:])
            w_ps = ps.tile([P, PACK, P], F32, name=f"w_ps{h}", tag=f"bankW{h}")
            for t in range(PACK):
                nc.tensor.matmul_mx(
                    out=w_ps[:, t, :],
                    lhsT=u_codes[t].bitcast(E4M3), lhsT_scale=u_plane[t],
                    rhs=g_codes[:].bitcast(E5M2), rhs_scale=g_plane[:],
                    start=True, stop=True,
                )
            return w_ps

        def round_moment(h, w_ps):
            w_bf = sb.tile([P, P, PACK], BF16, name=f"w_bf{h}", align_bytes=64)
            nc.scalar.copy(out=w_bf[:], in_=w_ps[:].rearrange("p t n -> p n t"))
            return w_bf

        def second_product(h, w_bf):
            w_codes = sb.tile([P, P], U32, name=f"w_codes{h}", align_bytes=64)
            w_plane = sb.tile([P, P], U8, name=f"w_plane{h}", align_bytes=64)
            nc.vector.quantize_mx(
                out=w_codes[:].bitcast(E5M2), scales=w_plane[:], in_=w_bf[:].rearrange("p n t -> p (n t)")
            )
            v_ps = ps.tile([P, HALVES, P], F32, name=f"v_ps{h}", tag=f"bankX{h + 1}")
            for rh in range(HALVES):
                nc.tensor.matmul_mx(
                    out=v_ps[:, rh, :],
                    lhsT=dr_codes[:, rh * P : (rh + 1) * P].bitcast(E5M2), lhsT_scale=dr_plane[:, rh * P : (rh + 1) * P],
                    rhs=w_codes[:].bitcast(E5M2), rhs_scale=w_plane[:],
                    start=True, stop=True,
                )
            return v_ps

        out_rows = out.rearrange("(h p) n -> p h n", p=P)

        def store(h, v_ps):
            res = sb.tile([P, HALVES, P], F32, name=f"res{h}")
            nc.vector.scalar_tensor_tensor(
                out=res[:], in0=v_ps[:], scalar=0.05, in1=old_scaled[:, :, h * P : (h + 1) * P],
                op0=ALU.mult, op1=ALU.max,
            )
            nc.sync.dma_start(out=out_rows[:, :, h * P : (h + 1) * P], in_=res[:])

        pick_share(gt_pick[1], gt_sb[1], offs2_sb, GT1_COLS)
        gj0 = turn_gradients(0)
        gj1 = turn_gradients(1)
        quantize_features(1, "factor3")
        w_ps0 = first_product(0, gj0)
        old_scaled = sb.tile([P, HALVES, N], F32, name="old_scaled", tag="gj0", align_bytes=64)
        nc.vector.tensor_scalar(out=old_scaled[:], in0=old_sb[:], scalar1=0.05, scalar2=None, op0=ALU.mult)
        w_ps1 = first_product(1, gj1)
        w_bf0 = round_moment(0, w_ps0)
        w_bf1 = round_moment(1, w_ps1)
        v_ps0 = second_product(0, w_bf0)
        v_ps1 = second_product(1, w_bf1)
        store(0, v_ps0)
        store(1, v_ps1)
